import numpy as np
import ml_dtypes


def mxq(x, axis, fmt="e4m3"):
    dtype, down = {"e4m3": (ml_dtypes.float8_e4m3fn, 7), "e5m2": (ml_dtypes.float8_e5m2, 14)}[fmt]
    v = np.moveaxis(np.asarray(x, np.float32).astype(ml_dtypes.bfloat16).astype(np.float64), axis, -1)
    blocks = v.reshape(v.shape[:-1] + (-1, 32))
    amax = np.abs(blocks).max(-1, keepdims=True)
    byte = np.maximum(np.where(amax > 0, np.frexp(amax)[1] - 1 + 127, 0) - down, 1)
    scale = np.exp2(byte - 127.0)
    codes = (blocks / scale).astype(np.float32).astype(dtype).astype(np.float64)
    return np.moveaxis((codes * scale).reshape(v.shape), -1, axis)


WIDE = False


def mx_kscale(k):
    if not WIDE:
        return np.ones(k)
    levels = np.array([10, -10, 5, -5, 0])
    if k % 512:
        return np.exp2(np.random.permutation(np.resize(levels, k // 32))).repeat(32)
    a = np.empty((k // 512, 16))
    for p in range(k // 512):
        a[p, :8] = np.random.permutation(np.resize(levels, 8))
        for g in range(8):
            far = levels[np.abs(levels - a[p, g]) >= 10]
            a[p, g + 8] = far[np.random.randint(len(far))]
    return np.exp2(a.ravel()).repeat(32)


def f64(x):
    return np.asarray(x).astype(np.float64)


def striped(idx):
    return np.tile(idx.reshape(-1, 16).T, (8, 1)).astype(np.uint16)


def unstriped(offs):
    return offs[:16].T.reshape(-1).astype(np.int64)


def pack_weight(w):
    k, n = w.shape
    w = f64(np.asarray(w, np.float32).astype(ml_dtypes.bfloat16)).reshape(k // 32, 32, n)
    amax = np.abs(w).max(1)
    byte = np.clip(np.where(amax > 0, np.frexp(amax)[1] - 1 + 127 - 7, 1), 1, 254)
    scaled = (w * np.exp2(127.0 - byte)[:, None, :]).reshape(k, n).astype(np.float32)
    words = np.ascontiguousarray(scaled.reshape(k // 512, 128, 4, n).transpose(0, 1, 3, 2)).astype(ml_dtypes.float8_e4m3fn).view(np.uint8)
    return words, np.ascontiguousarray(byte.astype(np.uint8).reshape(k // 512, 16, n))


def unpack_weight(words, scales):
    g, p, n, _ = words.shape
    vals = np.ascontiguousarray(words).view(ml_dtypes.float8_e4m3fn).astype(np.float64) * np.repeat(np.exp2(scales.astype(np.float64) - 127.0), 8, axis=1)[..., None]
    return vals.transpose(0, 1, 3, 2).reshape(g * 512, n)


E2M1 = np.array([0.0, 0.5, 1.0, 1.5, 2.0, 3.0, 4.0, 6.0, -0.0, -0.5, -1.0, -1.5, -2.0, -3.0, -4.0, -6.0])


def pack_fp4(w):
    k, n = w.shape
    w = f64(np.asarray(w, np.float32).astype(ml_dtypes.bfloat16)).reshape(k // 32, 32, n)
    amax = np.abs(w).max(1)
    mant, ex = np.frexp(amax / 6.0)
    byte = np.clip(np.where(amax > 0, np.where(mant > 0.5, ex, ex - 1) + 127, 1), 1, 254)
    scaled = (w * np.exp2(127.0 - byte)[:, None, :]).reshape(k, n).astype(np.float32)
    c = np.ascontiguousarray(scaled.reshape(k // 512, 128, 4, n).transpose(0, 1, 3, 2)).astype(ml_dtypes.float4_e2m1fn).view(np.uint8) & 0xF
    words = (c[..., 0::2] | (c[..., 1::2] << 4)).reshape(k // 512, 128, 2 * n)
    return np.ascontiguousarray(words), np.ascontiguousarray(byte.astype(np.uint8).reshape(k // 512, 16, n))


def unpack_fp4(words, scales):
    g, _, n = scales.shape
    words = np.ascontiguousarray(words).reshape(g, 128, n, 2)
    nib = np.empty((g, 128, n, 4), np.uint8)
    nib[..., 0::2] = words & 0xF
    nib[..., 1::2] = words >> 4
    vals = E2M1[nib] * np.repeat(np.exp2(scales.astype(np.float64) - 127.0), 8, axis=1)[..., None]
    return vals.transpose(0, 1, 3, 2).reshape(g * 512, n)


K, T, S, N, H, U = 512, 1024, 512, 256, 512, 1024


def setup_inputs():
    n = np.random.standard_normal
    s = mx_kscale(K)[:, None]
    u = mx_kscale(H)
    packed_xT = pack_weight(n((K, T)) * s)
    packed_w1 = pack_fp4(n((K, H)) / np.sqrt(K) / s)
    packed_w2 = pack_fp4(n((H, N)) / np.sqrt(H) / u[:, None])
    return {
        "x_words": packed_xT[0],
        "x_scales": packed_xT[1],
        "w1_words": packed_w1[0],
        "w1_scales": packed_w1[1],
        "adv": (np.random.uniform(0.0, 0.5, (H, U))).astype(np.float32),
        "drw": (np.random.uniform(0.5, 1.5, (H, U))).astype(np.float32),
        "sc": (np.random.uniform(0.0, 1.0, (H, U))).astype(np.float32),
        "unit": (np.random.uniform(0.6, 1.4, (H, 1)) * u[:, None]).astype(np.float32),
        "w2_words": packed_w2[0],
        "w2_scales": packed_w2[1],
        "offs": striped(np.random.permutation(T)[:S]),
        "home": striped(np.random.permutation(np.concatenate([np.arange(S), np.random.randint(0, S, U - S)]))),
        "away": striped(np.random.permutation(np.concatenate([np.arange(S), np.random.randint(0, S, U - S)]))),
    }


def reference(x_words, x_scales, w1_words, w1_scales, adv, drw, sc, unit, w2_words, w2_scales, offs, home, away):
    xq = unpack_weight(x_words, x_scales)[:, unstriped(offs)]
    rt = unpack_fp4(w1_words, w1_scales).T @ xq
    rh = rt[:, unstriped(home)]
    ra = rt[:, unstriped(away)]
    dif = rh - ra + f64(adv)
    eh = np.exp(0.9 * np.tanh(dif))
    ea = np.exp(-0.9 * np.tanh(dif))
    ph = eh / (eh + ea + f64(drw))
    pd = f64(drw) / (eh + ea + f64(drw))
    gr = f64(sc) - ph - (0.5 * pd)
    hid = f64(unit) * (gr * dif - np.log(pd))
    return unpack_fp4(w2_words, w2_scales).T @ mxq(hid, 0, "e4m3")

@@ -1,0 +1,335 @@
+from contextlib import ExitStack
+
+import concourse.mybir as mybir
+from concourse.masks import make_identity
+
+K, T, S, N, H, U = 512, 1024, 512, 256, 512, 1024
+FLOPS = 2 * K * H * S + 2 * H * N * U
+
+F32 = mybir.dt.float32
+BF16 = mybir.dt.bfloat16
+I32 = mybir.dt.int32
+U32 = mybir.dt.uint32
+U16 = mybir.dt.uint16
+U8 = mybir.dt.uint8
+FP8X4 = mybir.dt.float8_e4m3fn_x4
+FP4X4 = mybir.dt.float4_e2m1fn_x4
+ACT = mybir.ActivationFunctionType
+ALU = mybir.AluOpType
+
+P = 128
+PLANES = 4
+CH = 512
+G = 256
+NB = U // P
+TH = [2,2]
+THB = 1
+CHUNKS = [5,3]
+N_PE = [0,1]
+X_PE = []
+L_AT = ["mid","end"]
+RT_V = [0]
+OUT_V = []
+UNITS = [2,2,2,1,1]
+CB = [[[5],[6],[3],[7,4]],[[5,6,3],[7,4],[5,6],[3,7]]]
+LB = [[0,1,2,3,4],[0,1,2]]
+OB = [0,1,2,0,1]
+
+
+def tile_picked_yelodr_log_p_kernel(
+    tc, x_words, x_scales, w1_words, w1_scales, adv, drw, sc, unit, w2_words, w2_scales, offs, home, away, out
+):
+    nc = tc.nc
+    with ExitStack() as ctx:
+        lists = ctx.enter_context(tc.tile_pool(name="lists", bufs=1))
+        keep = ctx.enter_context(tc.tile_pool(name="keep", bufs=1))
+        ring = ctx.enter_context(tc.tile_pool(name="ring", bufs=2))
+        psum = ctx.enter_context(tc.psum_pool(name="psum", bufs=1))
+
+        offs_t = lists.tile([P, S // 16], U16, name="offs_t")
+        home_t = lists.tile([P, U // 16], U16, name="home_t")
+        away_t = lists.tile([P, U // 16], U16, name="away_t")
+
+        xw = keep.tile([P, T], I32, name="xw", align_bytes=64)
+        xs = keep.tile([P, T], U8, name="xs", align_bytes=64)
+        w1w = keep.tile([P, 2 * H], U8, name="w1w", align_bytes=64)
+        w1s = keep.tile([P, H], U8, name="w1s", align_bytes=64)
+        w2w = keep.tile([P, 2 * N], U8, name="w2w", align_bytes=64)
+        w2s = keep.tile([P, N], U8, name="w2s", align_bytes=64)
+        unit_t = keep.tile([P, PLANES], F32, name="unit_t")
+        ident = keep.tile([P, P], F32, name="ident")
+
+        def load_scales(tile, scales):
+            for q in range(4):
+                nc.sync.dma_start(tile[32 * q : 32 * q + 4, :].bitcast(I32), scales[0, 4 * q : 4 * q + 4, :].bitcast(I32))
+
+        nc.vector.memset(xs[:].bitcast(I32), 0)
+        nc.gpsimd.memset(w1s[:].bitcast(I32), 0)
+        nc.gpsimd.memset(w2s[:].bitcast(I32), 0)
+        make_identity(nc, ident[:])
+        nc.sync.dma_start(offs_t[:], offs)
+        nc.sync.dma_start(xw[:], x_words[0].rearrange("p n t -> p (n t)").bitcast(I32))
+        nc.sync.dma_start(w1w[:].bitcast(I32), w1_words[0].bitcast(I32))
+        load_scales(xs, x_scales)
+        load_scales(w1s, w1_scales)
+        nc.sync.dma_start(away_t[:], away)
+        nc.sync.dma_start(home_t[:], home)
+
+        first = [sum(CHUNKS[:c]) for c in range(len(CHUNKS))]
+        width = [n * P for n in CHUNKS]
+
+        def planes_of(x, c):
+            return x.rearrange("(t p) r -> p t r", p=P)[:, :, first[c] * P : first[c] * P + width[c]]
+
+        adv_t = [keep.tile([P, PLANES, width[c]], F32, name=f"adv{c}", tag=f"adv{c}") for c in range(2)]
+        drw_t = [keep.tile([P, PLANES, width[c]], F32, name=f"drw{c}") for c in range(2)]
+        sc_t = [keep.tile([P, PLANES, width[c]], F32, name=f"sc{c}") for c in range(2)]
+        nc.sync.dma_start(adv_t[0][:, 0, :], planes_of(adv, 0)[:, 0, :])
+        nc.sync.dma_start(adv_t[0][:, 1, :], planes_of(adv, 0)[:, 1, :])
+        nc.sync.dma_start(drw_t[0][:], planes_of(drw, 0))
+        for t in range(2, PLANES):
+            nc.sync.dma_start(adv_t[0][:, t, :], planes_of(adv, 0)[:, t, :])
+        for t in range(PLANES):
+            nc.sync.dma_start(adv_t[1][:, t, :], planes_of(adv, 1)[:, t, :])
+        nc.sync.dma_start(drw_t[1][:], planes_of(drw, 1))
+        nc.sync.dma_start(unit_t[:], unit.rearrange("(p t) o -> p (t o)", t=PLANES))
+        nc.sync.dma_start(w2w[:].bitcast(I32), w2_words[0].bitcast(I32))
+        load_scales(w2s, w2_scales)
+        for c in range(2):
+            nc.sync.dma_start(sc_t[c][:], planes_of(sc, c))
+
+        xq = keep.tile([P, S], U32, name="xq", align_bytes=64)
+        xqs = keep.tile([P, S], U8, name="xqs", align_bytes=64)
+        nc.vector.tensor_copy(xq[:], xw[:].bitcast(U32).indirect(offs_t[:]))
+        nc.vector.tensor_copy(xqs[:], xs[:].indirect(offs_t[:]))
+
+        def bank_tile(n):
+            return psum.tile([P, CH], F32, name=f"bank{n}", tag=f"bank{n}")
+
+        rt = []
+        for t in range(PLANES):
+            bank = bank_tile(t)
+            nc.tensor.matmul_mx(
+                out=bank[:],
+                lhsT=w1w[:, 2 * P * t : 2 * P * (t + 1)].bitcast(FP4X4),
+                lhsT_scale=w1s[:, P * t : P * (t + 1)],
+                rhs=xq[:].bitcast(FP8X4),
+                rhs_scale=xqs[:],
+                start=True,
+                stop=True,
+            )
+            plane = keep.tile([P, S], F32, name=f"rt{t}", tag=f"rt{t}")
+            if t in RT_V:
+                nc.vector.tensor_copy(plane[:], bank[:])
+            else:
+                nc.scalar.copy(plane[:], bank[:])
+            rt.append(plane)
+
+        def turn_plane(bank, t, terms):
+            for n, term in enumerate(terms):
+                nc.tensor.matmul(
+                    bank[:, P * t : P * (t + 1)], term(t), ident[:], start=(n == 0), stop=(n == len(terms) - 1), is_transpose=True
+                )
+
+        def turn(bank, terms):
+            for t in range(PLANES):
+                turn_plane(bank, t, terms)
+
+        def a_block(tile, j):
+            return lambda t: tile[:, t, P * j : P * (j + 1)]
+
+        def b_block(tile):
+            return lambda t: tile[:, P * t : P * (t + 1)]
+
+        def dealt(bank):
+            return bank[:].rearrange("r (p t) -> r t p", t=PLANES)
+
+        def as_planes(ap):
+            return ap.rearrange("r (t p) -> r t p", t=PLANES)
+
+        dif = [keep.tile([P, PLANES, width[c]], F32, name=f"dif{c}") for c in range(2)]
+        eh = [keep.tile([P, PLANES, width[c]], F32, name=f"eh{c}") for c in range(2)]
+        ea = [keep.tile([P, PLANES, width[c]], F32, name=f"ea{c}") for c in range(2)]
+        hid = keep.tile([P, U * PLANES], BF16, name="hid", align_bytes=64)
+        hq = keep.tile([P, U], U32, name="hq", align_bytes=64)
+        hqs = keep.tile([P, U], U8, name="hqs", align_bytes=64)
+        ln_den = keep.tile([P, NB, CH], F32, name="ln_den")
+        ln_drw = keep.tile([P, NB, CH], F32, name="ln_drw")
+        rec = keep.tile([P, NB, CH], F32, name="rec")
+
+        def gathers(c):
+            pieces = [(a, min(a + G, width[c])) for a in range(0, width[c], G)]
+            for t in range(PLANES):
+                xa = [keep.tile([P, G], F32, name=f"xa{h}", tag=f"xa{h}") for h in range(len(pieces))]
+                for h, (a, b) in enumerate(pieces):
+                    cols = slice((first[c] * P + a) // 16, (first[c] * P + b) // 16)
+                    nc.vector.tensor_tensor(xa[h][:, : b - a], rt[t][:].indirect(away_t[:, cols]), adv_t[c][:, t, a:b], ALU.subtract)
+                for h, (a, b) in enumerate(pieces):
+                    cols = slice((first[c] * P + a) // 16, (first[c] * P + b) // 16)
+                    nc.vector.tensor_tensor(dif[c][:, t, a:b], rt[t][:].indirect(home_t[:, cols]), xa[h][:, : b - a], ALU.subtract)
+
+        def exps(c):
+            banks = [bank_tile(j) for j in range(CHUNKS[c])]
+            ths = []
+            for t in range(PLANES):
+                cuts = TH[c]
+                for h in range(cuts):
+                    a, b = h * width[c] // cuts, (h + 1) * width[c] // cuts
+                    th = keep.tile([P, b - a], F32, name=f"th{h}", tag=f"th{h}", bufs=THB)
+                    ths.append((th, a, b))
+                    nc.scalar.activation(th[:], dif[c][:, t, a:b], ACT.Tanh)
+                for th, a, b in ths[-cuts:]:
+                    nc.scalar.activation(eh[c][:, t, a:b], th[:], ACT.Exp, scale=0.9)
+                    nc.scalar.activation(ea[c][:, t, a:b], th[:], ACT.Exp, scale=-0.9)
+                for j in range(CHUNKS[c]):
+                    turn_plane(banks[j], t, [a_block(drw_t[c], j), a_block(eh[c], j), a_block(ea[c], j)])
+            return banks
+
+        def log_den(c, banks):
+            for j in range(CHUNKS[c]):
+                nc.scalar.activation(as_planes(ln_den[:, first[c] + j, :]), dealt(banks[j]), ACT.Ln)
+
+        def log_drw(c):
+            for j in range(CHUNKS[c]):
+                bank = bank_tile(LB[c][j % len(LB[c])])
+                turn(bank, [a_block(drw_t[c], j)])
+                nc.scalar.activation(as_planes(ln_drw[:, first[c] + j, :]), dealt(bank), ACT.Ln)
+
+        def recips(c):
+            for j in range(CHUNKS[c]):
+                nc.scalar.activation(rec[:, first[c] + j, :], ln_den[:, first[c] + j, :], ACT.Exp, scale=-1.0)
+
+        def side(c):
+            nlp = keep.tile([P, CHUNKS[c], CH], F32, name=f"nlp{c}", tag="adv1" if c == 0 else "adv0")
+            num = keep.tile([P, PLANES, width[c]], F32, name=f"num{c}", tag="rt3" if c == 0 else "rt2")
+            for j in range(CHUNKS[c]):
+                b = first[c] + j
+                if b not in N_PE:
+                    cols = slice(P * j, P * (j + 1))
+                    nc.gpsimd.tensor_tensor(num[:, :, cols], eh[c][:, :, cols], ea[c][:, :, cols], ALU.subtract)
+                if b in X_PE:
+                    nc.gpsimd.tensor_scalar(nlp[:, j, :], ln_drw[:, b, :], -1.0, 0.0, ALU.mult, ALU.add)
+                else:
+                    nc.gpsimd.tensor_tensor(nlp[:, j, :], ln_den[:, b, :], ln_drw[:, b, :], ALU.subtract)
+            return nlp, num
+
+        def chain_bank(c, k, j):
+            return bank_tile(CB[c][k][j % len(CB[c][k])])
+
+        def step_m(c, j, num):
+            bank = chain_bank(c, 0, j)
+            if first[c] + j in N_PE:
+                turn(bank, [a_block(drw_t[c], j), a_block(eh[c], j), a_block(eh[c], j)])
+            else:
+                turn(bank, [a_block(num, j)])
+            m = ring.tile([P, CH], F32, name="m")
+            nc.vector.scalar_tensor_tensor(as_planes(m[:]), dealt(bank), -0.5, as_planes(rec[:, first[c] + j, :]), ALU.mult, ALU.mult)
+            return m
+
+        def step_g(c, j, m):
+            bank = chain_bank(c, 1, j)
+            turn(bank, [a_block(sc_t[c], j)])
+            gr = ring.tile([P, CH], F32, name="gr")
+            nc.vector.scalar_tensor_tensor(as_planes(gr[:]), dealt(bank), 0.0 if first[c] + j in N_PE else -0.5, as_planes(m[:]), ALU.add, ALU.add)
+            return gr
+
+        def step_p(c, j, gr):
+            bank = chain_bank(c, 2, j)
+            turn(bank, [a_block(dif[c], j)])
+            pr = ring.tile([P, CH], F32, name="pr", bufs=2)
+            nc.vector.tensor_tensor(as_planes(pr[:]), dealt(bank), as_planes(gr[:]), ALU.mult)
+            return pr
+
+        def step_h(c, j, pr, nlp):
+            bank = chain_bank(c, 3, j)
+            b = first[c] + j
+            terms = [b_block(nlp[:, j, :])]
+            if b in X_PE:
+                terms.append(b_block(ln_den[:, b, :]))
+            terms.append(b_block(pr[:]))
+            turn(bank, terms)
+            nc.vector.tensor_tensor(
+                hid[:, b * CH : (b + 1) * CH].rearrange("p (r t) -> p r t", t=PLANES),
+                bank[:].rearrange("p (t r) -> p r t", t=PLANES),
+                unit_t[:].unsqueeze(1).to_broadcast([P, P, PLANES]),
+                ALU.mult,
+            )
+
+        ends = [sum(UNITS[: u + 1]) for u in range(len(UNITS))]
+
+        def unit_cols(u):
+            return slice((ends[u] - UNITS[u]) * P, ends[u] * P)
+
+        def quantise(u):
+            cols = unit_cols(u)
+            nc.vector.quantize_mx(out=hq[:, cols].bitcast(FP8X4), scales=hqs[:, cols], in_=hid[:, cols.start * PLANES : cols.stop * PLANES])
+
+        def product(u):
+            cols = unit_cols(u)
+            w = UNITS[u] * P
+            bank = bank_tile(OB[u])
+            for mt in range(N // P):
+                nc.tensor.matmul_mx(
+                    out=bank[:, mt * w : (mt + 1) * w],
+                    lhsT=w2w[:, 2 * P * mt : 2 * P * (mt + 1)].bitcast(FP4X4),
+                    lhsT_scale=w2s[:, P * mt : P * (mt + 1)],
+                    rhs=hq[:, cols].bitcast(FP8X4),
+                    rhs_scale=hqs[:, cols],
+                    start=True,
+                    stop=True,
+                )
+            res = keep.tile([P, N // P, w], F32, name=f"res{u}")
+            src = bank[:, : 2 * w].rearrange("p (m r) -> p m r", r=w)
+            if u in OUT_V:
+                nc.vector.tensor_copy(res[:], src)
+            else:
+                nc.scalar.copy(res[:], src)
+            nc.sync.dma_start(out.rearrange("(m p) r -> p m r", p=P)[:, :, cols], res[:])
+
+        def chain(c, num, nlp, now):
+            ms, grs, prs = {}, {}, {}
+            n = CHUNKS[c]
+            later = []
+            for step in range(n + 3):
+                if step < n:
+                    ms[step] = step_m(c, step, num)
+                if 0 <= step - 1 < n:
+                    grs[step - 1] = step_g(c, step - 1, ms[step - 1])
+                if 0 <= step - 2 < n:
+                    prs[step - 2] = step_p(c, step - 2, grs[step - 2])
+                if 0 <= step - 3 < n:
+                    j = step - 3
+                    step_h(c, j, prs[j], nlp)
+                    if first[c] + j + 1 in ends:
+                        u = ends.index(first[c] + j + 1)
+                        quantise(u)
+                        if now:
+                            product(u)
+                        else:
+                            later.append(u)
+            return later
+
+        for c in range(2):
+            if L_AT[c] == "head":
+                log_drw(c)
+        gathers(0)
+        banks0 = exps(0)
+        gathers(1)
+        log_den(0, banks0)
+        for c in range(2):
+            if L_AT[c] == "mid":
+                log_drw(c)
+        recips(0)
+        banks1 = exps(1)
+        nlp0, num0 = side(0)
+        later = chain(0, num0, nlp0, False)
+        log_den(1, banks1)
+        if L_AT[1] == "late":
+            log_drw(1)
+        recips(1)
+        if L_AT[1] == "end":
+            log_drw(1)
+        nlp1, num1 = side(1)
+        for u in later:
+            product(u)
+        chain(1, num1, nlp1, True)

@@ -22,18 +22,30 @@ PLANES = 4
 CH = 512
 G = 256
 NB = U // P
-TH = [2,2]
+OWE = [0,1]
+XF = [5,6,7]
+PRE = [[["s",0],["d",0],["s",1]],[]]
+CG = True
+N_V = [0,1,2]
+X_V = [0,1]
+ROT = [[0,1,2,3,4],[5,6,7,0,1,2,3,4]]
+NT = ["rt3","xa1","xa0"]
+EARLY = True
+ACC = [False,False]
+DB = [[0,1,2,3,4],[5,6,7]]
+RB = [7,6,5,4]
+TH = [2,1]
 THB = 1
 CHUNKS = [5,3]
-N_PE = [0,1]
+N_PE = []
 X_PE = []
-L_AT = ["mid","end"]
+L_AT = ["head","mid"]
 RT_V = [0]
 OUT_V = []
 UNITS = [2,2,2,1,1]
-CB = [[[5],[6],[3],[7,4]],[[5,6,3],[7,4],[5,6],[3,7]]]
-LB = [[0,1,2,3,4],[0,1,2]]
-OB = [0,1,2,0,1]
+CB = [[[0],[1],[2],[3,4]],[[0,5],[1,6],[2,7],[3,4]]]
+LB = [[0,1,2,3,4],[5,6,7]]
+OB = [5,6,7,0,1]
 
 
 def tile_picked_yelodr_log_p_kernel(
@@ -67,13 +79,6 @@ def tile_picked_yelodr_log_p_kernel(
         nc.gpsimd.memset(w1s[:].bitcast(I32), 0)
         nc.gpsimd.memset(w2s[:].bitcast(I32), 0)
         make_identity(nc, ident[:])
-        nc.sync.dma_start(offs_t[:], offs)
-        nc.sync.dma_start(xw[:], x_words[0].rearrange("p n t -> p (n t)").bitcast(I32))
-        nc.sync.dma_start(w1w[:].bitcast(I32), w1_words[0].bitcast(I32))
-        load_scales(xs, x_scales)
-        load_scales(w1s, w1_scales)
-        nc.sync.dma_start(away_t[:], away)
-        nc.sync.dma_start(home_t[:], home)
 
         first = [sum(CHUNKS[:c]) for c in range(len(CHUNKS))]
         width = [n * P for n in CHUNKS]
@@ -82,16 +87,35 @@ def tile_picked_yelodr_log_p_kernel(
             return x.rearrange("(t p) r -> p t r", p=P)[:, :, first[c] * P : first[c] * P + width[c]]
 
         adv_t = [keep.tile([P, PLANES, width[c]], F32, name=f"adv{c}", tag=f"adv{c}") for c in range(2)]
-        drw_t = [keep.tile([P, PLANES, width[c]], F32, name=f"drw{c}") for c in range(2)]
         sc_t = [keep.tile([P, PLANES, width[c]], F32, name=f"sc{c}") for c in range(2)]
+        drw_all = drw.rearrange("(t p) r -> p t r", p=P)
+        drw_b = {}
+
+        def load_drw(a, b, tag, planes=slice(0, PLANES)):
+            if a not in drw_b:
+                tile = keep.tile([P, PLANES, (b - a) * P], F32, name=f"drw{a}", tag=tag)
+                for j in range(a, b):
+                    drw_b[j] = (tile, j - a)
+            nc.sync.dma_start(drw_b[a][0][:, planes, :], drw_all[:, planes, a * P : b * P])
+
+        nc.sync.dma_start(offs_t[:], offs)
+        nc.sync.dma_start(xw[:], x_words[0].rearrange("p n t -> p (n t)").bitcast(I32))
+        nc.sync.dma_start(away_t[:], away)
+        load_drw(0, 1, "drw0", slice(0, 1))
+        nc.sync.dma_start(w1w[:].bitcast(I32), w1_words[0].bitcast(I32))
+        load_scales(xs, x_scales)
+        load_scales(w1s, w1_scales)
+        nc.sync.dma_start(home_t[:], home)
         nc.sync.dma_start(adv_t[0][:, 0, :], planes_of(adv, 0)[:, 0, :])
-        nc.sync.dma_start(adv_t[0][:, 1, :], planes_of(adv, 0)[:, 1, :])
-        nc.sync.dma_start(drw_t[0][:], planes_of(drw, 0))
-        for t in range(2, PLANES):
+        load_drw(0, 1, "drw0", slice(1, PLANES))
+        load_drw(1, 3, "drw1")
+        load_drw(3, 4, "th1")
+        load_drw(4, 5, "th0")
+        for t in range(1, PLANES):
             nc.sync.dma_start(adv_t[0][:, t, :], planes_of(adv, 0)[:, t, :])
+        load_drw(5, 8, "drw5")
         for t in range(PLANES):
             nc.sync.dma_start(adv_t[1][:, t, :], planes_of(adv, 1)[:, t, :])
-        nc.sync.dma_start(drw_t[1][:], planes_of(drw, 1))
         nc.sync.dma_start(unit_t[:], unit.rearrange("(p t) o -> p (t o)", t=PLANES))
         nc.sync.dma_start(w2w[:].bitcast(I32), w2_words[0].bitcast(I32))
         load_scales(w2s, w2_scales)
@@ -108,7 +132,7 @@ def tile_picked_yelodr_log_p_kernel(
 
         rt = []
         for t in range(PLANES):
-            bank = bank_tile(t)
+            bank = bank_tile(RB[t])
             nc.tensor.matmul_mx(
                 out=bank[:],
                 lhsT=w1w[:, 2 * P * t : 2 * P * (t + 1)].bitcast(FP4X4),
@@ -125,10 +149,10 @@ def tile_picked_yelodr_log_p_kernel(
                 nc.scalar.copy(plane[:], bank[:])
             rt.append(plane)
 
-        def turn_plane(bank, t, terms):
+        def turn_plane(bank, t, terms, fresh=True, last=True):
             for n, term in enumerate(terms):
                 nc.tensor.matmul(
-                    bank[:, P * t : P * (t + 1)], term(t), ident[:], start=(n == 0), stop=(n == len(terms) - 1), is_transpose=True
+                    bank[:, P * t : P * (t + 1)], term(t), ident[:], start=(fresh and n == 0), stop=(last and n == len(terms) - 1), is_transpose=True
                 )
 
         def turn(bank, terms):
@@ -157,6 +181,8 @@ def tile_picked_yelodr_log_p_kernel(
         ln_drw = keep.tile([P, NB, CH], F32, name="ln_drw")
         rec = keep.tile([P, NB, CH], F32, name="rec")
 
+        held = [[], []]
+
         def gathers(c):
             pieces = [(a, min(a + G, width[c])) for a in range(0, width[c], G)]
             for t in range(PLANES):
@@ -169,20 +195,29 @@ def tile_picked_yelodr_log_p_kernel(
                     nc.vector.tensor_tensor(dif[c][:, t, a:b], rt[t][:].indirect(home_t[:, cols]), xa[h][:, : b - a], ALU.subtract)
 
         def exps(c):
-            banks = [bank_tile(j) for j in range(CHUNKS[c])]
+            banks = [bank_tile(DB[c][j]) for j in range(CHUNKS[c])]
+            for j in range(CHUNKS[c]):
+                for t in range(PLANES):
+                    turn_plane(banks[j], t, [a_block(*drw_b[first[c] + j])], t == 0, False)
             ths = []
             for t in range(PLANES):
                 cuts = TH[c]
                 for h in range(cuts):
                     a, b = h * width[c] // cuts, (h + 1) * width[c] // cuts
-                    th = keep.tile([P, b - a], F32, name=f"th{h}", tag=f"th{h}", bufs=THB)
+                    th = keep.tile([P, b - a], F32, name=f"th{h}", tag=f"th{(h + t * cuts) % 2}", bufs=THB)
                     ths.append((th, a, b))
                     nc.scalar.activation(th[:], dif[c][:, t, a:b], ACT.Tanh)
                 for th, a, b in ths[-cuts:]:
                     nc.scalar.activation(eh[c][:, t, a:b], th[:], ACT.Exp, scale=0.9)
                     nc.scalar.activation(ea[c][:, t, a:b], th[:], ACT.Exp, scale=-0.9)
+                if CG and c == 1:
+                    both = ring.tile([P, 1, width[c]], F32, name="both")
+                    nc.gpsimd.tensor_tensor(both[:, 0, :], eh[c][:, t, :], ea[c][:, t, :], ALU.add)
                 for j in range(CHUNKS[c]):
-                    turn_plane(banks[j], t, [a_block(drw_t[c], j), a_block(eh[c], j), a_block(ea[c], j)])
+                    terms = [a_block(eh[c], j), a_block(ea[c], j)]
+                    if CG and c == 1:
+                        terms = [lambda t, j=j, both=both: both[:, 0, P * j : P * (j + 1)]]
+                    turn_plane(banks[j], t, terms, False, t == PLANES - 1)
             return banks
 
         def log_den(c, banks):
@@ -192,8 +227,13 @@ def tile_picked_yelodr_log_p_kernel(
         def log_drw(c):
             for j in range(CHUNKS[c]):
                 bank = bank_tile(LB[c][j % len(LB[c])])
-                turn(bank, [a_block(drw_t[c], j)])
-                nc.scalar.activation(as_planes(ln_drw[:, first[c] + j, :]), dealt(bank), ACT.Ln)
+                held[c].append(bank)
+                spans = [(0, 1), (1, PLANES)] if first[c] + j == 0 and EARLY else [(0, PLANES)]
+                for t0, t1 in spans:
+                    for t in range(t0, t1):
+                        turn_plane(bank, t, [a_block(*drw_b[first[c] + j])])
+                    part = slice(32 * t0, 32 * t1)
+                    nc.scalar.activation(as_planes(ln_drw[:, first[c] + j, :])[:, :, part], dealt(bank)[:, :, part], ACT.Ln)
 
         def recips(c):
             for j in range(CHUNKS[c]):
@@ -201,41 +241,50 @@ def tile_picked_yelodr_log_p_kernel(
 
         def side(c):
             nlp = keep.tile([P, CHUNKS[c], CH], F32, name=f"nlp{c}", tag="adv1" if c == 0 else "adv0")
-            num = keep.tile([P, PLANES, width[c]], F32, name=f"num{c}", tag="rt3" if c == 0 else "rt2")
+            num = {}
             for j in range(CHUNKS[c]):
                 b = first[c] + j
                 if b not in N_PE:
                     cols = slice(P * j, P * (j + 1))
-                    nc.gpsimd.tensor_tensor(num[:, :, cols], eh[c][:, :, cols], ea[c][:, :, cols], ALU.subtract)
+                    num[j] = keep.tile([P, PLANES, P], F32, name=f"num{b}", tag=NT[b % len(NT)])
+                    (nc.vector if b in N_V else nc.gpsimd).tensor_tensor(num[j][:], eh[c][:, :, cols], ea[c][:, :, cols], ALU.subtract)
                 if b in X_PE:
                     nc.gpsimd.tensor_scalar(nlp[:, j, :], ln_drw[:, b, :], -1.0, 0.0, ALU.mult, ALU.add)
                 else:
-                    nc.gpsimd.tensor_tensor(nlp[:, j, :], ln_den[:, b, :], ln_drw[:, b, :], ALU.subtract)
+                    (nc.vector if b in X_V else nc.gpsimd).tensor_tensor(nlp[:, j, :], ln_den[:, b, :], ln_drw[:, b, :], ALU.subtract)
             return nlp, num
 
+        turns = [0, 0]
+
         def chain_bank(c, k, j):
-            return bank_tile(CB[c][k][j % len(CB[c][k])])
+            turns[c] += 1
+            return bank_tile(ROT[c][(turns[c] - 1) % len(ROT[c])])
+
+        early = {}
+
+        def flip(c, k, j, tile):
+            bank = chain_bank(c, k, j)
+            turn(bank, [a_block(tile, j)])
+            return bank
 
         def step_m(c, j, num):
             bank = chain_bank(c, 0, j)
             if first[c] + j in N_PE:
-                turn(bank, [a_block(drw_t[c], j), a_block(eh[c], j), a_block(eh[c], j)])
+                turn(bank, [a_block(*drw_b[first[c] + j]), a_block(eh[c], j), a_block(eh[c], j)])
             else:
-                turn(bank, [a_block(num, j)])
+                turn(bank, [a_block(num[j], 0)])
             m = ring.tile([P, CH], F32, name="m")
             nc.vector.scalar_tensor_tensor(as_planes(m[:]), dealt(bank), -0.5, as_planes(rec[:, first[c] + j, :]), ALU.mult, ALU.mult)
             return m
 
         def step_g(c, j, m):
-            bank = chain_bank(c, 1, j)
-            turn(bank, [a_block(sc_t[c], j)])
+            bank = early.pop(("s", c, j), None) or flip(c, 1, j, sc_t[c])
             gr = ring.tile([P, CH], F32, name="gr")
             nc.vector.scalar_tensor_tensor(as_planes(gr[:]), dealt(bank), 0.0 if first[c] + j in N_PE else -0.5, as_planes(m[:]), ALU.add, ALU.add)
             return gr
 
         def step_p(c, j, gr):
-            bank = chain_bank(c, 2, j)
-            turn(bank, [a_block(dif[c], j)])
+            bank = early.pop(("d", c, j), None) or flip(c, 2, j, dif[c])
             pr = ring.tile([P, CH], F32, name="pr", bufs=2)
             nc.vector.tensor_tensor(as_planes(pr[:]), dealt(bank), as_planes(gr[:]), ALU.mult)
             return pr
@@ -243,11 +292,16 @@ def tile_picked_yelodr_log_p_kernel(
         def step_h(c, j, pr, nlp):
             bank = chain_bank(c, 3, j)
             b = first[c] + j
-            terms = [b_block(nlp[:, j, :])]
+            terms = [b_block(pr[:]), b_block(nlp[:, j, :])]
             if b in X_PE:
                 terms.append(b_block(ln_den[:, b, :]))
-            terms.append(b_block(pr[:]))
-            turn(bank, terms)
+            if b in XF:
+                for t in range(PLANES):
+                    turn_plane(bank, t, terms[1:], t == 0, False)
+                for t in range(PLANES):
+                    turn_plane(bank, t, terms[:1], False, t == PLANES - 1)
+            else:
+                turn(bank, terms)
             nc.vector.tensor_tensor(
                 hid[:, b * CH : (b + 1) * CH].rearrange("p (r t) -> p r t", t=PLANES),
                 bank[:].rearrange("p (t r) -> p r t", t=PLANES),
@@ -267,7 +321,7 @@ def tile_picked_yelodr_log_p_kernel(
         def product(u):
             cols = unit_cols(u)
             w = UNITS[u] * P
-            bank = bank_tile(OB[u])
+            bank = chain_bank(1, 0, 0)
             for mt in range(N // P):
                 nc.tensor.matmul_mx(
                     out=bank[:, mt * w : (mt + 1) * w],
@@ -286,11 +340,15 @@ def tile_picked_yelodr_log_p_kernel(
                 nc.scalar.copy(res[:], src)
             nc.sync.dma_start(out.rearrange("(m p) r -> p m r", p=P)[:, :, cols], res[:])
 
-        def chain(c, num, nlp, now):
+        def chain(c, num, nlp, now, owed=()):
             ms, grs, prs = {}, {}, {}
             n = CHUNKS[c]
             later = []
+            for kind, j in PRE[c]:
+                early[kind, c, j] = flip(c, 0, j, sc_t[c] if kind == "s" else dif[c])
             for step in range(n + 3):
+                if step in OWE and owed:
+                    product(owed[OWE.index(step)])
                 if step < n:
                     ms[step] = step_m(c, step, num)
                 if 0 <= step - 1 < n:
@@ -330,6 +388,4 @@ def tile_picked_yelodr_log_p_kernel(
         if L_AT[1] == "end":
             log_drw(1)
         nlp1, num1 = side(1)
-        for u in later:
-            product(u)
-        chain(1, num1, nlp1, True)
+        chain(1, num1, nlp1, True, later)

@@ -84,11 +84,11 @@ def tile_picked_yelodr_log_p_kernel(
         width = [n * P for n in CHUNKS]
 
         def planes_of(x, c):
-            return x.rearrange("(t p) r -> p t r", p=P)[:, :, first[c] * P : first[c] * P + width[c]]
+            return x.rearrange("(p t) r -> p t r", t=PLANES)[:, :, first[c] * P : first[c] * P + width[c]]
 
         adv_t = [keep.tile([P, PLANES, width[c]], F32, name=f"adv{c}", tag=f"adv{c}") for c in range(2)]
         sc_t = [keep.tile([P, PLANES, width[c]], F32, name=f"sc{c}") for c in range(2)]
-        drw_all = drw.rearrange("(t p) r -> p t r", p=P)
+        drw_all = drw.rearrange("(p t) r -> p t r", t=PLANES)
         drw_b = {}
 
         def load_drw(a, b, tag, planes=slice(0, PLANES)):
@@ -127,6 +127,12 @@ def tile_picked_yelodr_log_p_kernel(
         nc.vector.tensor_copy(xq[:], xw[:].bitcast(U32).indirect(offs_t[:]))
         nc.vector.tensor_copy(xqs[:], xs[:].indirect(offs_t[:]))
 
+        w1p = keep.tile([P, 2 * H], U8, name="w1p", align_bytes=64)
+        w1q = keep.tile([P, H], U8, name="w1q", align_bytes=64)
+        nc.scalar.copy(w1p[:].bitcast(U16).rearrange("p (t m) -> p t m", t=PLANES), w1w[:].bitcast(U16).rearrange("p (m t) -> p t m", t=PLANES))
+        for t0, t1 in ((0, 1), (1, PLANES)):
+            nc.vector.tensor_copy(w1q[:].rearrange("p (t m) -> p t m", t=PLANES)[:, t0:t1, :], w1s[:].rearrange("p (m t) -> p t m", t=PLANES)[:, t0:t1, :])
+
         def bank_tile(n):
             return psum.tile([P, CH], F32, name=f"bank{n}", tag=f"bank{n}")
 
@@ -135,8 +141,8 @@ def tile_picked_yelodr_log_p_kernel(
             bank = bank_tile(RB[t])
             nc.tensor.matmul_mx(
                 out=bank[:],
-                lhsT=w1w[:, 2 * P * t : 2 * P * (t + 1)].bitcast(FP4X4),
-                lhsT_scale=w1s[:, P * t : P * (t + 1)],
+                lhsT=w1p[:, 2 * P * t : 2 * P * (t + 1)].bitcast(FP4X4),
+                lhsT_scale=w1q[:, P * t : P * (t + 1)],
                 rhs=xq[:].bitcast(FP8X4),
                 rhs_scale=xqs[:],
                 start=True,
@@ -166,10 +172,10 @@ def tile_picked_yelodr_log_p_kernel(
             return lambda t: tile[:, P * t : P * (t + 1)]
 
         def dealt(bank):
-            return bank[:].rearrange("r (p t) -> r t p", t=PLANES)
+            return bank[:]
 
         def as_planes(ap):
-            return ap.rearrange("r (t p) -> r t p", t=PLANES)
+            return ap
 
         dif = [keep.tile([P, PLANES, width[c]], F32, name=f"dif{c}") for c in range(2)]
         eh = [keep.tile([P, PLANES, width[c]], F32, name=f"eh{c}") for c in range(2)]
@@ -232,8 +238,8 @@ def tile_picked_yelodr_log_p_kernel(
                 for t0, t1 in spans:
                     for t in range(t0, t1):
                         turn_plane(bank, t, [a_block(*drw_b[first[c] + j])])
-                    part = slice(32 * t0, 32 * t1)
-                    nc.scalar.activation(as_planes(ln_drw[:, first[c] + j, :])[:, :, part], dealt(bank)[:, :, part], ACT.Ln)
+                    part = slice(P * t0, P * t1)
+                    nc.scalar.activation(ln_drw[:, first[c] + j, part], bank[:, part], ACT.Ln)
 
         def recips(c):
             for j in range(CHUNKS[c]):

from contextlib import ExitStack

import concourse.mybir as mybir
from concourse.masks import make_identity

K, T, S, N, H, U = 512, 1024, 512, 256, 512, 1024
FLOPS = 2 * K * H * S + 2 * H * N * U

F32 = mybir.dt.float32
BF16 = mybir.dt.bfloat16
I32 = mybir.dt.int32
U32 = mybir.dt.uint32
U16 = mybir.dt.uint16
U8 = mybir.dt.uint8
FP8X4 = mybir.dt.float8_e4m3fn_x4
FP4X4 = mybir.dt.float4_e2m1fn_x4
ACT = mybir.ActivationFunctionType
ALU = mybir.AluOpType

P = 128
PLANES = 4
CH = 512
G = 256
NB = U // P
OWE = [0,1]
XF = [5,6,7]
PRE = [[["s",0],["d",0],["s",1]],[]]
CG = True
N_V = [0,1,2]
X_V = [0,1]
ROT = [[0,1,2,3,4],[5,6,7,0,1,2,3,4]]
NT = ["rt3","xa1","xa0"]
EARLY = True
ACC = [False,False]
DB = [[0,1,2,3,4],[5,6,7]]
RB = [7,6,5,4]
TH = [2,1]
THB = 1
CHUNKS = [5,3]
N_PE = []
X_PE = []
L_AT = ["head","mid"]
RT_V = [0]
OUT_V = []
UNITS = [2,2,2,1,1]
CB = [[[0],[1],[2],[3,4]],[[0,5],[1,6],[2,7],[3,4]]]
LB = [[0,1,2,3,4],[5,6,7]]
OB = [5,6,7,0,1]


def tile_picked_yelodr_log_p_kernel(
    tc, x_words, x_scales, w1_words, w1_scales, adv, drw, sc, unit, w2_words, w2_scales, offs, home, away, out
):
    nc = tc.nc
    with ExitStack() as ctx:
        lists = ctx.enter_context(tc.tile_pool(name="lists", bufs=1))
        keep = ctx.enter_context(tc.tile_pool(name="keep", bufs=1))
        ring = ctx.enter_context(tc.tile_pool(name="ring", bufs=2))
        psum = ctx.enter_context(tc.psum_pool(name="psum", bufs=1))

        offs_t = lists.tile([P, S // 16], U16, name="offs_t")
        home_t = lists.tile([P, U // 16], U16, name="home_t")
        away_t = lists.tile([P, U // 16], U16, name="away_t")

        xw = keep.tile([P, T], I32, name="xw", align_bytes=64)
        xs = keep.tile([P, T], U8, name="xs", align_bytes=64)
        w1w = keep.tile([P, 2 * H], U8, name="w1w", align_bytes=64)
        w1s = keep.tile([P, H], U8, name="w1s", align_bytes=64)
        w2w = keep.tile([P, 2 * N], U8, name="w2w", align_bytes=64)
        w2s = keep.tile([P, N], U8, name="w2s", align_bytes=64)
        unit_t = keep.tile([P, PLANES], F32, name="unit_t")
        ident = keep.tile([P, P], F32, name="ident")

        def load_scales(tile, scales):
            for q in range(4):
                nc.sync.dma_start(tile[32 * q : 32 * q + 4, :].bitcast(I32), scales[0, 4 * q : 4 * q + 4, :].bitcast(I32))

        nc.vector.memset(xs[:].bitcast(I32), 0)
        nc.gpsimd.memset(w1s[:].bitcast(I32), 0)
        nc.gpsimd.memset(w2s[:].bitcast(I32), 0)
        make_identity(nc, ident[:])

        first = [sum(CHUNKS[:c]) for c in range(len(CHUNKS))]
        width = [n * P for n in CHUNKS]

        def planes_of(x, c):
            return x.rearrange("(p t) r -> p t r", t=PLANES)[:, :, first[c] * P : first[c] * P + width[c]]

        adv_t = [keep.tile([P, PLANES, width[c]], F32, name=f"adv{c}", tag=f"adv{c}") for c in range(2)]
        sc_t = [keep.tile([P, PLANES, width[c]], F32, name=f"sc{c}") for c in range(2)]
        drw_all = drw.rearrange("(p t) r -> p t r", t=PLANES)
        drw_b = {}

        def load_drw(a, b, tag, planes=slice(0, PLANES)):
            if a not in drw_b:
                tile = keep.tile([P, PLANES, (b - a) * P], F32, name=f"drw{a}", tag=tag)
                for j in range(a, b):
                    drw_b[j] = (tile, j - a)
            nc.sync.dma_start(drw_b[a][0][:, planes, :], drw_all[:, planes, a * P : b * P])

        nc.sync.dma_start(offs_t[:], offs)
        nc.sync.dma_start(xw[:], x_words[0].rearrange("p n t -> p (n t)").bitcast(I32))
        nc.sync.dma_start(away_t[:], away)
        load_drw(0, 1, "drw0", slice(0, 1))
        nc.sync.dma_start(w1w[:].bitcast(I32), w1_words[0].bitcast(I32))
        load_scales(xs, x_scales)
        load_scales(w1s, w1_scales)
        nc.sync.dma_start(home_t[:], home)
        nc.sync.dma_start(adv_t[0][:, 0, :], planes_of(adv, 0)[:, 0, :])
        load_drw(0, 1, "drw0", slice(1, PLANES))
        load_drw(1, 3, "drw1")
        load_drw(3, 4, "th1")
        load_drw(4, 5, "th0")
        for t in range(1, PLANES):
            nc.sync.dma_start(adv_t[0][:, t, :], planes_of(adv, 0)[:, t, :])
        load_drw(5, 8, "drw5")
        for t in range(PLANES):
            nc.sync.dma_start(adv_t[1][:, t, :], planes_of(adv, 1)[:, t, :])
        nc.sync.dma_start(unit_t[:], unit.rearrange("(p t) o -> p (t o)", t=PLANES))
        nc.sync.dma_start(w2w[:].bitcast(I32), w2_words[0].bitcast(I32))
        load_scales(w2s, w2_scales)
        for c in range(2):
            nc.sync.dma_start(sc_t[c][:], planes_of(sc, c))

        xq = keep.tile([P, S], U32, name="xq", align_bytes=64)
        xqs = keep.tile([P, S], U8, name="xqs", align_bytes=64)
        nc.vector.tensor_copy(xq[:], xw[:].bitcast(U32).indirect(offs_t[:]))
        nc.vector.tensor_copy(xqs[:], xs[:].indirect(offs_t[:]))

        w1p = keep.tile([P, 2 * H], U8, name="w1p", align_bytes=64)
        w1q = keep.tile([P, H], U8, name="w1q", align_bytes=64)
        nc.scalar.copy(w1p[:].bitcast(U16).rearrange("p (t m) -> p t m", t=PLANES), w1w[:].bitcast(U16).rearrange("p (m t) -> p t m", t=PLANES))
        for t0, t1 in ((0, 1), (1, PLANES)):
            nc.vector.tensor_copy(w1q[:].rearrange("p (t m) -> p t m", t=PLANES)[:, t0:t1, :], w1s[:].rearrange("p (m t) -> p t m", t=PLANES)[:, t0:t1, :])

        def bank_tile(n):
            return psum.tile([P, CH], F32, name=f"bank{n}", tag=f"bank{n}")

        rt = []
        for t in range(PLANES):
            bank = bank_tile(RB[t])
            nc.tensor.matmul_mx(
                out=bank[:],
                lhsT=w1p[:, 2 * P * t : 2 * P * (t + 1)].bitcast(FP4X4),
                lhsT_scale=w1q[:, P * t : P * (t + 1)],
                rhs=xq[:].bitcast(FP8X4),
                rhs_scale=xqs[:],
                start=True,
                stop=True,
            )
            plane = keep.tile([P, S], F32, name=f"rt{t}", tag=f"rt{t}")
            if t in RT_V:
                nc.vector.tensor_copy(plane[:], bank[:])
            else:
                nc.scalar.copy(plane[:], bank[:])
            rt.append(plane)

        def turn_plane(bank, t, terms, fresh=True, last=True):
            for n, term in enumerate(terms):
                nc.tensor.matmul(
                    bank[:, P * t : P * (t + 1)], term(t), ident[:], start=(fresh and n == 0), stop=(last and n == len(terms) - 1), is_transpose=True
                )

        def turn(bank, terms):
            for t in range(PLANES):
                turn_plane(bank, t, terms)

        def a_block(tile, j):
            return lambda t: tile[:, t, P * j : P * (j + 1)]

        def b_block(tile):
            return lambda t: tile[:, P * t : P * (t + 1)]

        def dealt(bank):
            return bank[:]

        def as_planes(ap):
            return ap

        dif = [keep.tile([P, PLANES, width[c]], F32, name=f"dif{c}") for c in range(2)]
        eh = [keep.tile([P, PLANES, width[c]], F32, name=f"eh{c}") for c in range(2)]
        ea = [keep.tile([P, PLANES, width[c]], F32, name=f"ea{c}") for c in range(2)]
        hid = keep.tile([P, U * PLANES], BF16, name="hid", align_bytes=64)
        hq = keep.tile([P, U], U32, name="hq", align_bytes=64)
        hqs = keep.tile([P, U], U8, name="hqs", align_bytes=64)
        ln_den = keep.tile([P, NB, CH], F32, name="ln_den")
        ln_drw = keep.tile([P, NB, CH], F32, name="ln_drw")
        rec = keep.tile([P, NB, CH], F32, name="rec")

        held = [[], []]

        def gathers(c):
            pieces = [(a, min(a + G, width[c])) for a in range(0, width[c], G)]
            for t in range(PLANES):
                xa = [keep.tile([P, G], F32, name=f"xa{h}", tag=f"xa{h}") for h in range(len(pieces))]
                for h, (a, b) in enumerate(pieces):
                    cols = slice((first[c] * P + a) // 16, (first[c] * P + b) // 16)
                    nc.vector.tensor_tensor(xa[h][:, : b - a], rt[t][:].indirect(away_t[:, cols]), adv_t[c][:, t, a:b], ALU.subtract)
                for h, (a, b) in enumerate(pieces):
                    cols = slice((first[c] * P + a) // 16, (first[c] * P + b) // 16)
                    nc.vector.tensor_tensor(dif[c][:, t, a:b], rt[t][:].indirect(home_t[:, cols]), xa[h][:, : b - a], ALU.subtract)

        def exps(c):
            banks = [bank_tile(DB[c][j]) for j in range(CHUNKS[c])]
            for j in range(CHUNKS[c]):
                for t in range(PLANES):
                    turn_plane(banks[j], t, [a_block(*drw_b[first[c] + j])], t == 0, False)
            ths = []
            for t in range(PLANES):
                cuts = TH[c]
                for h in range(cuts):
                    a, b = h * width[c] // cuts, (h + 1) * width[c] // cuts
                    th = keep.tile([P, b - a], F32, name=f"th{h}", tag=f"th{(h + t * cuts) % 2}", bufs=THB)
                    ths.append((th, a, b))
                    nc.scalar.activation(th[:], dif[c][:, t, a:b], ACT.Tanh)
                for th, a, b in ths[-cuts:]:
                    nc.scalar.activation(eh[c][:, t, a:b], th[:], ACT.Exp, scale=0.9)
                    nc.scalar.activation(ea[c][:, t, a:b], th[:], ACT.Exp, scale=-0.9)
                if CG and c == 1:
                    both = ring.tile([P, 1, width[c]], F32, name="both")
                    nc.gpsimd.tensor_tensor(both[:, 0, :], eh[c][:, t, :], ea[c][:, t, :], ALU.add)
                for j in range(CHUNKS[c]):
                    terms = [a_block(eh[c], j), a_block(ea[c], j)]
                    if CG and c == 1:
                        terms = [lambda t, j=j, both=both: both[:, 0, P * j : P * (j + 1)]]
                    turn_plane(banks[j], t, terms, False, t == PLANES - 1)
            return banks

        def log_den(c, banks):
            for j in range(CHUNKS[c]):
                nc.scalar.activation(as_planes(ln_den[:, first[c] + j, :]), dealt(banks[j]), ACT.Ln)

        def log_drw(c):
            for j in range(CHUNKS[c]):
                bank = bank_tile(LB[c][j % len(LB[c])])
                held[c].append(bank)
                spans = [(0, 1), (1, PLANES)] if first[c] + j == 0 and EARLY else [(0, PLANES)]
                for t0, t1 in spans:
                    for t in range(t0, t1):
                        turn_plane(bank, t, [a_block(*drw_b[first[c] + j])])
                    part = slice(P * t0, P * t1)
                    nc.scalar.activation(ln_drw[:, first[c] + j, part], bank[:, part], ACT.Ln)

        def recips(c):
            for j in range(CHUNKS[c]):
                nc.scalar.activation(rec[:, first[c] + j, :], ln_den[:, first[c] + j, :], ACT.Exp, scale=-1.0)

        def side(c):
            nlp = keep.tile([P, CHUNKS[c], CH], F32, name=f"nlp{c}", tag="adv1" if c == 0 else "adv0")
            num = {}
            for j in range(CHUNKS[c]):
                b = first[c] + j
                if b not in N_PE:
                    cols = slice(P * j, P * (j + 1))
                    num[j] = keep.tile([P, PLANES, P], F32, name=f"num{b}", tag=NT[b % len(NT)])
                    (nc.vector if b in N_V else nc.gpsimd).tensor_tensor(num[j][:], eh[c][:, :, cols], ea[c][:, :, cols], ALU.subtract)
                if b in X_PE:
                    nc.gpsimd.tensor_scalar(nlp[:, j, :], ln_drw[:, b, :], -1.0, 0.0, ALU.mult, ALU.add)
                else:
                    (nc.vector if b in X_V else nc.gpsimd).tensor_tensor(nlp[:, j, :], ln_den[:, b, :], ln_drw[:, b, :], ALU.subtract)
            return nlp, num

        turns = [0, 0]

        def chain_bank(c, k, j):
            turns[c] += 1
            return bank_tile(ROT[c][(turns[c] - 1) % len(ROT[c])])

        early = {}

        def flip(c, k, j, tile):
            bank = chain_bank(c, k, j)
            turn(bank, [a_block(tile, j)])
            return bank

        def step_m(c, j, num):
            bank = chain_bank(c, 0, j)
            if first[c] + j in N_PE:
                turn(bank, [a_block(*drw_b[first[c] + j]), a_block(eh[c], j), a_block(eh[c], j)])
            else:
                turn(bank, [a_block(num[j], 0)])
            m = ring.tile([P, CH], F32, name="m")
            nc.vector.scalar_tensor_tensor(as_planes(m[:]), dealt(bank), -0.5, as_planes(rec[:, first[c] + j, :]), ALU.mult, ALU.mult)
            return m

        def step_g(c, j, m):
            bank = early.pop(("s", c, j), None) or flip(c, 1, j, sc_t[c])
            gr = ring.tile([P, CH], F32, name="gr")
            nc.vector.scalar_tensor_tensor(as_planes(gr[:]), dealt(bank), 0.0 if first[c] + j in N_PE else -0.5, as_planes(m[:]), ALU.add, ALU.add)
            return gr

        def step_p(c, j, gr):
            bank = early.pop(("d", c, j), None) or flip(c, 2, j, dif[c])
            pr = ring.tile([P, CH], F32, name="pr", bufs=2)
            nc.vector.tensor_tensor(as_planes(pr[:]), dealt(bank), as_planes(gr[:]), ALU.mult)
            return pr

        def step_h(c, j, pr, nlp):
            bank = chain_bank(c, 3, j)
            b = first[c] + j
            terms = [b_block(pr[:]), b_block(nlp[:, j, :])]
            if b in X_PE:
                terms.append(b_block(ln_den[:, b, :]))
            if b in XF:
                for t in range(PLANES):
                    turn_plane(bank, t, terms[1:], t == 0, False)
                for t in range(PLANES):
                    turn_plane(bank, t, terms[:1], False, t == PLANES - 1)
            else:
                turn(bank, terms)
            nc.vector.tensor_tensor(
                hid[:, b * CH : (b + 1) * CH].rearrange("p (r t) -> p r t", t=PLANES),
                bank[:].rearrange("p (t r) -> p r t", t=PLANES),
                unit_t[:].unsqueeze(1).to_broadcast([P, P, PLANES]),
                ALU.mult,
            )

        ends = [sum(UNITS[: u + 1]) for u in range(len(UNITS))]

        def unit_cols(u):
            return slice((ends[u] - UNITS[u]) * P, ends[u] * P)

        def quantise(u):
            cols = unit_cols(u)
            nc.vector.quantize_mx(out=hq[:, cols].bitcast(FP8X4), scales=hqs[:, cols], in_=hid[:, cols.start * PLANES : cols.stop * PLANES])

        def product(u):
            cols = unit_cols(u)
            w = UNITS[u] * P
            bank = chain_bank(1, 0, 0)
            for mt in range(N // P):
                nc.tensor.matmul_mx(
                    out=bank[:, mt * w : (mt + 1) * w],
                    lhsT=w2w[:, 2 * P * mt : 2 * P * (mt + 1)].bitcast(FP4X4),
                    lhsT_scale=w2s[:, P * mt : P * (mt + 1)],
                    rhs=hq[:, cols].bitcast(FP8X4),
                    rhs_scale=hqs[:, cols],
                    start=True,
                    stop=True,
                )
            res = keep.tile([P, N // P, w], F32, name=f"res{u}")
            src = bank[:, : 2 * w].rearrange("p (m r) -> p m r", r=w)
            if u in OUT_V:
                nc.vector.tensor_copy(res[:], src)
            else:
                nc.scalar.copy(res[:], src)
            nc.sync.dma_start(out.rearrange("(m p) r -> p m r", p=P)[:, :, cols], res[:])

        def chain(c, num, nlp, now, owed=()):
            ms, grs, prs = {}, {}, {}
            n = CHUNKS[c]
            later = []
            for kind, j in PRE[c]:
                early[kind, c, j] = flip(c, 0, j, sc_t[c] if kind == "s" else dif[c])
            for step in range(n + 3):
                if step in OWE and owed:
                    product(owed[OWE.index(step)])
                if step < n:
                    ms[step] = step_m(c, step, num)
                if 0 <= step - 1 < n:
                    grs[step - 1] = step_g(c, step - 1, ms[step - 1])
                if 0 <= step - 2 < n:
                    prs[step - 2] = step_p(c, step - 2, grs[step - 2])
                if 0 <= step - 3 < n:
                    j = step - 3
                    step_h(c, j, prs[j], nlp)
                    if first[c] + j + 1 in ends:
                        u = ends.index(first[c] + j + 1)
                        quantise(u)
                        if now:
                            product(u)
                        else:
                            later.append(u)
            return later

        for c in range(2):
            if L_AT[c] == "head":
                log_drw(c)
        gathers(0)
        banks0 = exps(0)
        gathers(1)
        log_den(0, banks0)
        for c in range(2):
            if L_AT[c] == "mid":
                log_drw(c)
        recips(0)
        banks1 = exps(1)
        nlp0, num0 = side(0)
        later = chain(0, num0, nlp0, False)
        log_den(1, banks1)
        if L_AT[1] == "late":
            log_drw(1)
        recips(1)
        if L_AT[1] == "end":
            log_drw(1)
        nlp1, num1 = side(1)
        chain(1, num1, nlp1, True, later)
